import numpy as np
import ml_dtypes


def mxq(x, axis, fmt="e4m3"):
    dtype, down = {"e4m3": (ml_dtypes.float8_e4m3fn, 7), "e5m2": (ml_dtypes.float8_e5m2, 14)}[fmt]
    v = np.moveaxis(np.asarray(x, np.float32).astype(ml_dtypes.bfloat16).astype(np.float64), axis, -1)
    blocks = v.reshape(v.shape[:-1] + (-1, 32))
    amax = np.abs(blocks).max(-1, keepdims=True)
    byte = np.maximum(np.where(amax > 0, np.frexp(amax)[1] - 1 + 127, 0) - down, 1)
    scale = np.exp2(byte - 127.0)
    codes = (blocks / scale).astype(np.float32).astype(dtype).astype(np.float64)
    return np.moveaxis((codes * scale).reshape(v.shape), -1, axis)


WIDE = False


def mx_kscale(k):
    if not WIDE:
        return np.ones(k)
    levels = np.array([10, -10, 5, -5, 0])
    if k % 512:
        return np.exp2(np.random.permutation(np.resize(levels, k // 32))).repeat(32)
    a = np.empty((k // 512, 16))
    for p in range(k // 512):
        a[p, :8] = np.random.permutation(np.resize(levels, 8))
        for g in range(8):
            far = levels[np.abs(levels - a[p, g]) >= 10]
            a[p, g + 8] = far[np.random.randint(len(far))]
    return np.exp2(a.ravel()).repeat(32)


def f64(x):
    return np.asarray(x).astype(np.float64)


def striped(idx):
    return np.tile(idx.reshape(-1, 16).T, (8, 1)).astype(np.uint16)


def unstriped(offs):
    return offs[:16].T.reshape(-1).astype(np.int64)


E2M1 = np.array([0.0, 0.5, 1.0, 1.5, 2.0, 3.0, 4.0, 6.0, -0.0, -0.5, -1.0, -1.5, -2.0, -3.0, -4.0, -6.0])


def pack_weight(w, fmt):
    k, n = w.shape
    w = f64(np.asarray(w, np.float32).astype(ml_dtypes.bfloat16)).reshape(k // 32, 32, n)
    amax = np.abs(w).max(1)
    if fmt == "e4m3":
        byte = np.frexp(amax)[1] - 1 + 127 - 7
    else:
        mant, ex = np.frexp(amax / 6.0)
        byte = np.where(mant > 0.5, ex, ex - 1) + 127
    byte = np.clip(np.where(amax > 0, byte, 1), 1, 254)
    scaled = (w * np.exp2(127.0 - byte)[:, None, :]).reshape(k, n).astype(np.float32)
    by_word = np.ascontiguousarray(scaled.reshape(k // 512, 128, 4, n).transpose(0, 1, 3, 2))
    if fmt == "e4m3":
        words = by_word.astype(ml_dtypes.float8_e4m3fn).view(np.uint8)
    else:
        c = by_word.astype(ml_dtypes.float4_e2m1fn).view(np.uint8) & 0xF
        words = (c[..., 0::2] | (c[..., 1::2] << 4)).reshape(k // 512, 128, 2 * n)
    return np.ascontiguousarray(words), np.ascontiguousarray(byte.astype(np.uint8).reshape(k // 512, 16, n))


def unpack_weight(words, scales, fmt):
    g, _, n = scales.shape
    words = np.ascontiguousarray(words).reshape(g, 128, n, -1)
    if fmt == "e4m3":
        vals = words.view(ml_dtypes.float8_e4m3fn).astype(np.float64)
    else:
        nib = np.empty((g, 128, n, 4), np.uint8)
        nib[..., 0::2] = words & 0xF
        nib[..., 1::2] = words >> 4
        vals = E2M1[nib]
    vals = vals * np.repeat(np.exp2(scales.astype(np.float64) - 127.0), 8, axis=1)[..., None]
    return vals.transpose(0, 1, 3, 2).reshape(g * 512, n)


def gelu(v):
    return 0.5 * v * (1.0 + np.tanh(np.sqrt(2.0 / np.pi) * (v + 0.044715 * v**3)))


K, H, T, S, T2, P = 1536, 512, 2048, 1024, 2048, 1024


def setup_inputs():
    n = np.random.standard_normal
    s, u = mx_kscale(K)[:, None], mx_kscale(H)[:, None]
    d = {}
    d["tab_words"], d["tab_scales"] = pack_weight(n((K, T)) * s, "e4m3")
    d["offs"] = striped(np.random.permutation(T)[:S])
    d["offs2"] = striped(np.random.permutation(T2)[:S])
    d["offs3"] = striped(np.random.permutation(T2)[:P])
    d["offs4"] = striped(np.random.permutation(T2)[:P])
    d["w1_words"], d["w1_scales"] = pack_weight(1.4 * n((K, H)) / K**0.5 / s, "e2m1")
    d["w2"] = (1.2 * n((K, H)) / K**0.5 / s * u.T).astype(np.float32)
    d["tide"] = (0.6 * n((H, S)) * u).astype(np.float32)
    d["page0"] = (n((H, T2)) * u).astype(np.float32)
    d["wgs"] = np.exp(0.3 * n((128, S))).astype(np.float32)
    d["bather"] = np.exp(0.4 * n(H)).astype(np.float32)
    d["w3"] = (2.2 * n((H, H)) / H**0.5 / u).astype(np.float32)
    d["bar"] = (1.5 * np.exp(0.3 * n(H)) / u[:, 0]).astype(np.float32)
    return d


def reference(tab_words, tab_scales, offs, offs2, offs3, offs4, w1_words, w1_scales, w2, tide, page0, wgs, bather, w3, bar):
    v = unpack_weight(tab_words, tab_scales, "e4m3")[:, unstriped(offs)]
    a = unpack_weight(w1_words, w1_scales, "e2m1").T @ v
    b = mxq(f64(w2), 0, "e4m3").T @ v
    h = np.tanh(a) * b + f64(tide)
    page = f64(page0).copy()
    page[:, unstriped(offs2)] = np.tile(f64(wgs), (H // 128, 1)) * h
    x = np.abs(f64(bather)[:, None] * page[:, unstriped(offs3)])
    y = mxq(f64(w3), 0, "e4m3").T @ mxq(x, 0, "e4m3")
    sand = f64(bar)[:, None] * page[:, unstriped(offs4)]
    return y * (1.0 / (1.0 + np.exp(-sand))) + sand

@@ -1,0 +1,260 @@
+from contextlib import ExitStack
+
+import concourse.mybir as mybir
+from concourse.masks import make_identity
+
+K, H, T, S, T2, M = 1536, 512, 2048, 1024, 2048, 1024
+FLOPS = 2 * (2 * K * H * S) + 2 * H * H * M
+
+F32 = mybir.dt.float32
+BF16 = mybir.dt.bfloat16
+I32 = mybir.dt.int32
+U32 = mybir.dt.uint32
+U16 = mybir.dt.uint16
+U8 = mybir.dt.uint8
+FP8X4 = mybir.dt.float8_e4m3fn_x4
+FP4X4 = mybir.dt.float4_e2m1fn_x4
+ACT = mybir.ActivationFunctionType
+ALU = mybir.AluOpType
+
+P = 128
+PACK = 4
+PASSES = K // (P * PACK)
+BANK = 512
+HALVES = S // BANK
+JT = S // P
+
+
+def tile_list_rip_lookout_board_kernel(
+    tc, tab_words, tab_scales, offs, offs2, offs3, offs4, w1_words, w1_scales, w2, tide, page0, wgs, bather, w3, bar, out
+):
+    nc = tc.nc
+    with ExitStack() as ctx:
+        lists = ctx.enter_context(tc.tile_pool(name="lists", bufs=1))
+        sb = ctx.enter_context(tc.tile_pool(name="sb", bufs=1))
+        psum = ctx.enter_context(tc.psum_pool(name="psum", bufs=4))
+
+        idx1 = lists.tile([P, S // 16], U16, name="idx1")
+        idx2 = lists.tile([P, S // 16], U16, name="idx2")
+        idx3 = lists.tile([P, M // 16], U16, name="idx3")
+        idx4 = lists.tile([P, M // 16], U16, name="idx4")
+
+        tab_s = sb.tile([P, T], U8, name="tab_s", align_bytes=64)
+        w1_s = sb.tile([P, PASSES, H], U8, name="w1_s", align_bytes=64)
+        v_s = [sb.tile([P, S], U8, name="v_s%d" % a, align_bytes=64) for a in range(PASSES)]
+        nc.gpsimd.memset(tab_s[:].bitcast(I32), 0)
+        nc.gpsimd.memset(w1_s[:].bitcast(I32), 0)
+        for a in range(1, PASSES):
+            nc.vector.memset(v_s[a][:].bitcast(I32), 0)
+
+        nc.sync.dma_start(idx1[:], offs)
+        for q in range(4):
+            nc.scalar.dma_start(
+                out=tab_s[32 * q : 32 * q + 4 * PASSES, :].bitcast(I32),
+                in_=tab_scales[:, 4 * q : 4 * q + 4, :].bitcast(I32),
+            )
+        bather_c = sb.tile([P, PACK], F32, name="bather_c")
+        bar_c = sb.tile([P, PACK], F32, name="bar_c")
+        ident = sb.tile([P, P], F32, name="ident")
+        make_identity(nc, ident[:])
+
+        tab_w = [sb.tile([P, T], I32, name="tab_w%d" % a, align_bytes=64) for a in range(PASSES)]
+        w1_w = sb.tile([P, PASSES, 2 * H], U8, name="w1_w", align_bytes=64)
+
+        def load_table(a):
+            nc.sync.dma_start(out=tab_w[a][:], in_=tab_words[a].rearrange("p n i -> p (n i)").bitcast(I32))
+
+        load_table(0)
+        load_table(1)
+        nc.sync.dma_start(out=w1_w[:].bitcast(I32), in_=w1_words.rearrange("a p n -> p a n").bitcast(I32))
+        for q in range(4):
+            nc.gpsimd.dma_start(
+                out=w1_s[32 * q : 32 * q + 4, :, :].bitcast(I32),
+                in_=w1_scales[:, 4 * q : 4 * q + 4, :].rearrange("a r n -> r a n").bitcast(I32),
+            )
+        load_table(2)
+
+        def load_weight(rows, name):
+            raw = sb.tile([P, PACK, H], F32, name=name, tag="w_raw", bufs=3)
+            nc.sync.dma_start(out=raw[:], in_=rows.rearrange("(p i) c -> p i c", i=PACK))
+            return raw
+
+        tide_rows = tide.rearrange("(p t) j -> t p j", t=PACK)
+        early = sb.tile([P, PACK + 1, S], F32, name="early", tag="early_or_reread")
+        tide_sb = [early[:, t, :] for t in range(PACK)]
+        w2_raw = []
+        for a in range(PASSES):
+            if a == PASSES - 1:
+                nc.sync.dma_start(out=tide_sb[0], in_=tide_rows[0])
+            w2_raw.append(load_weight(w2[512 * a : 512 * (a + 1), :], "w2_raw%d" % a))
+
+        nc.sync.dma_start(idx2[:], offs2)
+        page_rows = page0.rearrange("(p t) c -> t p c", t=PACK)
+        wgs_rows = wgs.rearrange("(i u e) j -> u i e j", u=2, e=2)
+        page, wgs_sb = [], []
+        for t in range(PACK):
+            if t > 0:
+                nc.sync.dma_start(out=tide_sb[t], in_=tide_rows[t])
+            page.append(sb.tile([P, T2], F32, name="page%d" % t))
+            nc.sync.dma_start(out=page[t][:], in_=page_rows[t])
+            if t % 2 == 0:
+                pair = sb.tile([P, 2, S], F32, name="wgs%d" % t)
+                for q in range(4):
+                    nc.sync.dma_start(out=pair[32 * q : 32 * q + 32, :, :], in_=wgs_rows[t // 2])
+                wgs_sb.extend([pair[:, 0, :], pair[:, 1, :]])
+            if t == 1:
+                nc.sync.dma_start(idx3[:], offs3)
+                nc.sync.dma_start(idx4[:], offs4)
+                nc.sync.dma_start(out=bather_c[:], in_=bather.rearrange("(p t) -> p t", t=PACK))
+                nc.sync.dma_start(out=bar_c[:], in_=bar.rearrange("(p t) -> p t", t=PACK))
+        w3_raw = load_weight(w3, "w3_raw")
+
+        nc.vector.tensor_copy(v_s[0][:], tab_s[:].indirect(idx1[:]))
+        for a in range(1, PASSES):
+            nc.scalar.dma_start(out=v_s[a][0:100, :].bitcast(I32), in_=v_s[0][4 * a : 4 * a + 100, :].bitcast(I32))
+        v_w = [sb.tile([P, S], U32, name="v_w%d" % a, align_bytes=64) for a in range(PASSES)]
+        for a in range(PASSES - 1):
+            nc.vector.tensor_copy(v_w[a][:], tab_w[a][:].bitcast(U32).indirect(idx1[:]))
+        for half in range(HALVES):
+            nc.vector.tensor_copy(
+                v_w[PASSES - 1][:, half * BANK : (half + 1) * BANK],
+                tab_w[PASSES - 1][:].bitcast(U32).indirect(idx1[:, half * 32 : (half + 1) * 32]),
+            )
+
+        def first_product(jt, w_codes, w_scales, tag):
+            acc = psum.tile([P, BANK], F32, name="acc", tag=tag)
+            cols = slice(jt * P, (jt + 1) * P)
+            for a in range(PASSES):
+                nc.tensor.matmul_mx(
+                    out=acc[:],
+                    lhsT=v_w[a][:, cols].bitcast(FP8X4),
+                    lhsT_scale=v_s[a][:, cols],
+                    rhs=w_codes[a],
+                    rhs_scale=w_scales[a],
+                    start=(a == 0),
+                    stop=(a == PASSES - 1),
+                )
+            return acc
+
+        u = []
+        for jt in range(JT):
+            acc = first_product(
+                jt, [w1_w[:, a, :].bitcast(FP4X4) for a in range(PASSES)], [w1_s[:, a, :] for a in range(PASSES)], "bank_a"
+            )
+            u.append(sb.tile([P, PACK, P], F32, name="u%d" % jt, tag="u_or_out", bufs=JT))
+            nc.scalar.activation(u[jt][:], acc[:].rearrange("p (m t) -> p t m", t=PACK), ACT.Tanh)
+
+        w2_codes, w2_scales = [], []
+        for a in range(PASSES):
+            grouped = sb.tile([P, H, PACK], BF16, name="w2_bf%d" % a, tag="w_bf", bufs=3, align_bytes=64)
+            dst = grouped[:].rearrange("p (c e) i -> p c i e", e=4)
+            src = w2_raw[a][:].rearrange("p i (c e) -> p c i e", e=4)
+            nc.vector.tensor_copy(dst, src)
+            codes = sb.tile([P, H], U32, name="w2_q%d" % a, align_bytes=64)
+            scales = sb.tile([P, H], U8, name="w2_s%d" % a, align_bytes=64)
+            nc.vector.quantize_mx(
+                out=codes[:].bitcast(FP8X4), scales=scales[:], in_=grouped[:].rearrange("p c i -> p (c i)")
+            )
+            w2_codes.append(codes[:].bitcast(FP8X4))
+            w2_scales.append(scales[:])
+
+        for jt in range(JT):
+            acc = first_product(jt, w2_codes, w2_scales, "bank_b")
+            nc.vector.tensor_tensor(u[jt][:], acc[:].rearrange("p (m t) -> p t m", t=PACK), u[jt][:], ALU.mult)
+
+        def make_h(t):
+            h = early[:, PACK, :] if t == PACK - 1 else sb.tile([P, S], F32, name="h%d" % t)[:]
+            for half in range(HALVES):
+                turned = psum.tile([P, 4, P], F32, name="turned", tag="bank_a")
+                for b in range(4):
+                    jt = 4 * half + b
+                    nc.tensor.transpose(turned[:, b, :], tide_sb[t][:, jt * P : (jt + 1) * P], ident[:])
+                tide_t = sb.tile([P, 4, P], F32, name="tide_t", tag="tide_t_or_gate", bufs=8)
+                nc.scalar.copy(tide_t[:], turned[:])
+                acc = psum.tile([P, 4, P], F32, name="acc_h", tag="bank_a")
+                for b in range(4):
+                    jt = 4 * half + b
+                    nc.tensor.matmul(acc[:, b, :], u[jt][:, t, :], ident[:], start=True, stop=False, is_transpose=True)
+                    nc.tensor.matmul(acc[:, b, :], tide_t[:, b, :], ident[:], start=False, stop=True, is_transpose=True)
+                nc.scalar.copy(h[:, half * BANK : (half + 1) * BANK], acc[:].rearrange("p b j -> p (b j)"))
+            return h
+
+        def scatter(t):
+            h = make_h(t)
+            pieces = HALVES if t == 0 else 1
+            width = S // pieces
+            for i in range(pieces):
+                cols = slice(i * width, (i + 1) * width)
+                offsets = idx2[:, i * width // 16 : (i + 1) * width // 16]
+                nc.vector.tensor_tensor(page[t][:].indirect(offsets), h[:, cols], wgs_sb[t][:, cols], ALU.mult)
+
+        x = [sb.tile([P, BANK, PACK], BF16, name="x%d" % half, tag="x%d" % half, align_bytes=64) for half in range(HALVES)]
+        sandbar = [None] * PACK
+        gate = {}
+
+        def reread_bathers(t):
+            cells = reread[:, t, :]
+            for half in range(HALVES):
+                cols = slice(half * BANK, (half + 1) * BANK)
+                nc.vector.tensor_copy(cells[:, cols], page[t][:].indirect(idx3[:, half * 32 : (half + 1) * 32]))
+                nc.scalar.activation(x[half][:, :, t], cells[:, cols], ACT.Abs, scale=bather_c[:, t : t + 1])
+
+        def reread_sandbar(t):
+            if t < PACK - 1:
+                sandbar[t] = reread[:, PACK + t, :]
+            else:
+                sandbar[t] = sb.tile([P, M], F32, name="sandbar", tag="x0", align_bytes=64)[:]
+            nc.vector.tensor_copy(sandbar[t], page[t][:].indirect(idx4[:]))
+            for half in range(HALVES):
+                gate[t, half] = sb.tile([P, BANK], F32, name="gate", tag="tide_t_or_gate", bufs=8)
+                nc.scalar.activation(
+                    gate[t, half][:], sandbar[t][:, half * BANK : (half + 1) * BANK], ACT.Sigmoid, scale=bar_c[:, t : t + 1]
+                )
+
+        for t in range(PACK):
+            scatter(t)
+
+        w3_bf = sb.tile([P, PACK, P, PACK], BF16, name="w3_bf", tag="w_bf", bufs=3, align_bytes=64)
+        nc.scalar.copy(w3_bf[:].rearrange("p t m i -> p m t i"), w3_raw[:].rearrange("p i (m t) -> p m t i", t=PACK))
+        w3_q = sb.tile([P, H], U32, name="w3_q", align_bytes=64)
+        w3_s = sb.tile([P, H], U8, name="w3_s", align_bytes=64)
+        nc.vector.quantize_mx(
+            out=w3_q[:].bitcast(FP8X4), scales=w3_s[:], in_=w3_bf[:].rearrange("p t m i -> p (t m i)")
+        )
+
+        reread = sb.tile([P, 2 * PACK - 1, M], F32, name="reread", tag="early_or_reread")
+        for t in range(PACK):
+            reread_bathers(t)
+        for t in range(PACK - 1):
+            reread_sandbar(t)
+
+        out_rows = out.rearrange("(p t) m -> t p m", t=PACK)
+        x_q, x_s = [], []
+        for half in range(HALVES):
+            x_q.append(sb.tile([P, BANK], U32, name="x_q%d" % half, align_bytes=64))
+            x_s.append(sb.tile([P, BANK], U8, name="x_s%d" % half, align_bytes=64))
+            nc.vector.quantize_mx(
+                out=x_q[half][:].bitcast(FP8X4), scales=x_s[half][:], in_=x[half][:].rearrange("p m t -> p (m t)")
+            )
+        reread_sandbar(PACK - 1)
+        for half in range(HALVES):
+            cols = slice(half * BANK, (half + 1) * BANK)
+            res = []
+            for t in range(PACK):
+                y = psum.tile([P, BANK], F32, name="y", tag="bank_b")
+                nc.tensor.matmul_mx(
+                    out=y[:],
+                    lhsT=w3_q[:, t * P : (t + 1) * P].bitcast(FP8X4),
+                    lhsT_scale=w3_s[:, t * P : (t + 1) * P],
+                    rhs=x_q[half][:].bitcast(FP8X4),
+                    rhs_scale=x_s[half][:],
+                    start=True,
+                    stop=True,
+                )
+                res.append(sb.tile([P, BANK], F32, name="res", tag="u_or_out", bufs=JT))
+                nc.vector.tensor_tensor(res[t][:], y[:], gate[t, half][:], ALU.mult)
+                for done in ([t - 1] if t > 0 else []) + ([t] if t == PACK - 1 else []):
+                    nc.vector.scalar_tensor_tensor(
+                        res[done][:], sandbar[done][:, cols], bar_c[:, done : done + 1], res[done][:], ALU.mult, ALU.add
+                    )
+                    nc.sync.dma_start(out=out_rows[done][:, cols], in_=res[done][:])

@@ -22,7 +22,8 @@ PACK = 4
 PASSES = K // (P * PACK)
 BANK = 512
 HALVES = S // BANK
-JT = S // P
+BLOCKS = BANK // P
+LIST_COLS = BANK // 16
 
 
 def tile_list_rip_lookout_board_kernel(
@@ -39,6 +40,12 @@ def tile_list_rip_lookout_board_kernel(
         idx3 = lists.tile([P, M // 16], U16, name="idx3")
         idx4 = lists.tile([P, M // 16], U16, name="idx4")
 
+        def half_cols(half):
+            return slice(half * BANK, (half + 1) * BANK)
+
+        def half_list(idx, half):
+            return idx[:, half * LIST_COLS : (half + 1) * LIST_COLS]
+
         tab_s = sb.tile([P, T], U8, name="tab_s", align_bytes=64)
         w1_s = sb.tile([P, PASSES, H], U8, name="w1_s", align_bytes=64)
         v_s = [sb.tile([P, S], U8, name="v_s%d" % a, align_bytes=64) for a in range(PASSES)]
@@ -47,172 +54,183 @@ def tile_list_rip_lookout_board_kernel(
         for a in range(1, PASSES):
             nc.vector.memset(v_s[a][:].bitcast(I32), 0)
 
-        nc.sync.dma_start(idx1[:], offs)
-        for q in range(4):
-            nc.scalar.dma_start(
-                out=tab_s[32 * q : 32 * q + 4 * PASSES, :].bitcast(I32),
-                in_=tab_scales[:, 4 * q : 4 * q + 4, :].bitcast(I32),
-            )
-        bather_c = sb.tile([P, PACK], F32, name="bather_c")
-        bar_c = sb.tile([P, PACK], F32, name="bar_c")
-        ident = sb.tile([P, P], F32, name="ident")
-        make_identity(nc, ident[:])
-
         tab_w = [sb.tile([P, T], I32, name="tab_w%d" % a, align_bytes=64) for a in range(PASSES)]
         w1_w = sb.tile([P, PASSES, 2 * H], U8, name="w1_w", align_bytes=64)
 
         def load_table(a):
             nc.sync.dma_start(out=tab_w[a][:], in_=tab_words[a].rearrange("p n i -> p (n i)").bitcast(I32))
 
-        load_table(0)
-        load_table(1)
-        nc.sync.dma_start(out=w1_w[:].bitcast(I32), in_=w1_words.rearrange("a p n -> p a n").bitcast(I32))
-        for q in range(4):
-            nc.gpsimd.dma_start(
-                out=w1_s[32 * q : 32 * q + 4, :, :].bitcast(I32),
-                in_=w1_scales[:, 4 * q : 4 * q + 4, :].rearrange("a r n -> r a n").bitcast(I32),
-            )
-        load_table(2)
-
         def load_weight(rows, name):
-            raw = sb.tile([P, PACK, H], F32, name=name, tag="w_raw", bufs=3)
+            raw = sb.tile([P, PACK, H], F32, name=name, tag="w_raw", bufs=2)
             nc.sync.dma_start(out=raw[:], in_=rows.rearrange("(p i) c -> p i c", i=PACK))
             return raw
 
-        tide_rows = tide.rearrange("(p t) j -> t p j", t=PACK)
-        early = sb.tile([P, PACK + 1, S], F32, name="early", tag="early_or_reread")
-        tide_sb = [early[:, t, :] for t in range(PACK)]
-        w2_raw = []
-        for a in range(PASSES):
-            if a == PASSES - 1:
-                nc.sync.dma_start(out=tide_sb[0], in_=tide_rows[0])
-            w2_raw.append(load_weight(w2[512 * a : 512 * (a + 1), :], "w2_raw%d" % a))
+        nc.sync.dma_start(idx1[:], offs)
+        load_table(0)
+        for q in range(4):
+            queue = nc.scalar if q < 2 else nc.sync
+            queue.dma_start(
+                out=tab_s[32 * q : 32 * q + 4 * PASSES, :].bitcast(I32),
+                in_=tab_scales[:, 4 * q : 4 * q + 4, :].bitcast(I32),
+            )
+        load_table(1)
+        load_table(2)
+        nc.sync.dma_start(out=w1_w[:].bitcast(I32), in_=w1_words.rearrange("a p n -> p a n").bitcast(I32))
+        for q in range(4):
+            nc.sync.dma_start(
+                out=w1_s[32 * q : 32 * q + 4, :, :].bitcast(I32),
+                in_=w1_scales[:, 4 * q : 4 * q + 4, :].rearrange("a r n -> r a n").bitcast(I32),
+            )
+        w2_raw = [load_weight(w2[512 * a : 512 * (a + 1), :], "w2_raw%d" % a) for a in range(1)]
+        ident = sb.tile([P, P], F32, name="ident")
+        make_identity(nc, ident[:])
 
-        nc.sync.dma_start(idx2[:], offs2)
-        page_rows = page0.rearrange("(p t) c -> t p c", t=PACK)
-        wgs_rows = wgs.rearrange("(i u e) j -> u i e j", u=2, e=2)
-        page, wgs_sb = [], []
-        for t in range(PACK):
-            if t > 0:
-                nc.sync.dma_start(out=tide_sb[t], in_=tide_rows[t])
-            page.append(sb.tile([P, T2], F32, name="page%d" % t))
-            nc.sync.dma_start(out=page[t][:], in_=page_rows[t])
-            if t % 2 == 0:
-                pair = sb.tile([P, 2, S], F32, name="wgs%d" % t)
-                for q in range(4):
-                    nc.sync.dma_start(out=pair[32 * q : 32 * q + 32, :, :], in_=wgs_rows[t // 2])
-                wgs_sb.extend([pair[:, 0, :], pair[:, 1, :]])
-            if t == 1:
-                nc.sync.dma_start(idx3[:], offs3)
-                nc.sync.dma_start(idx4[:], offs4)
-                nc.sync.dma_start(out=bather_c[:], in_=bather.rearrange("(p t) -> p t", t=PACK))
-                nc.sync.dma_start(out=bar_c[:], in_=bar.rearrange("(p t) -> p t", t=PACK))
-        w3_raw = load_weight(w3, "w3_raw")
+        v_w = {}
 
+        def gather_words(a, half, tag):
+            v_w[a, half] = sb.tile([P, BANK], U32, name="v_w", tag=tag, align_bytes=64)
+            nc.vector.tensor_copy(v_w[a, half][:], tab_w[a][:].bitcast(U32).indirect(half_list(idx1, half)))
+
+        gather_words(0, 0, "v_w00")
         nc.vector.tensor_copy(v_s[0][:], tab_s[:].indirect(idx1[:]))
         for a in range(1, PASSES):
-            nc.scalar.dma_start(out=v_s[a][0:100, :].bitcast(I32), in_=v_s[0][4 * a : 4 * a + 100, :].bitcast(I32))
-        v_w = [sb.tile([P, S], U32, name="v_w%d" % a, align_bytes=64) for a in range(PASSES)]
-        for a in range(PASSES - 1):
-            nc.vector.tensor_copy(v_w[a][:], tab_w[a][:].bitcast(U32).indirect(idx1[:]))
-        for half in range(HALVES):
-            nc.vector.tensor_copy(
-                v_w[PASSES - 1][:, half * BANK : (half + 1) * BANK],
-                tab_w[PASSES - 1][:].bitcast(U32).indirect(idx1[:, half * 32 : (half + 1) * 32]),
-            )
+            for half in range(HALVES):
+                gather_words(a, half, "v_w%d%d" % (a, half))
+        for a in range(1, PASSES):
+            nc.sync.dma_start(out=v_s[a][0:100, :].bitcast(I32), in_=v_s[0][4 * a : 4 * a + 100, :].bitcast(I32))
 
-        def first_product(jt, w_codes, w_scales, tag):
+        tide_rows = tide.rearrange("(p t) j -> p t j", t=PACK)
+        page_rows = page0.rearrange("(p t) c -> t p c", t=PACK)
+        wgs_rows = wgs.rearrange("(i t) j -> i t j", t=PACK)
+        page = [sb.tile([P, T2], F32, name="page%d" % t) for t in range(PACK)]
+        tide_sb, wgs_sb = {}, {}
+
+        def load_tide(half, tile):
+            tide_sb[half] = tile.rearrange("p (t j) -> p t j", t=PACK)
+            nc.sync.dma_start(out=tide_sb[half], in_=tide_rows[:, :, half_cols(half)])
+
+        def load_page(t):
+            nc.sync.dma_start(out=page[t][:], in_=page_rows[t])
+
+        def load_wgs(half, t0, t1):
+            tile = sb.tile([P, t1 - t0, BANK], F32, name="wgs%d_%d" % (half, t0))
+            for q in range(4):
+                nc.sync.dma_start(out=tile[32 * q : 32 * q + 32, :, :], in_=wgs_rows[:, t0:t1, half_cols(half)])
+            for t in range(t0, t1):
+                wgs_sb[t, half] = tile[:, t - t0, :]
+
+        w2_raw.append(load_weight(w2[512:1024, :], "w2_raw1"))
+        last_raw = []
+        for c in range(2):
+            last_raw.append(sb.tile([P, PACK, H // 2], F32, name="w2_last%d" % c))
+            nc.sync.dma_start(
+                out=last_raw[c][:], in_=w2[1024:1536, c * H // 2 : (c + 1) * H // 2].rearrange("(p i) c -> p i c", i=PACK)
+            )
+        load_tide(0, sb.tile([P, PACK * BANK], F32, name="tide_first")[:])
+        nc.sync.dma_start(idx2[:], offs2)
+        load_page(0)
+        load_wgs(0, 0, 2)
+        load_page(1)
+        load_wgs(0, 2, 4)
+        load_page(2)
+        load_page(3)
+        early = sb.tile([P, 2 * PACK * BANK], F32, name="early", tag="early_or_reread")
+        load_tide(1, early[:, 0 : PACK * BANK])
+        load_wgs(1, 0, 4)
+        bather_c = sb.tile([P, PACK], F32, name="bather_c")
+        bar_c = sb.tile([P, PACK], F32, name="bar_c")
+        nc.sync.dma_start(idx3[:], offs3)
+        nc.sync.dma_start(idx4[:], offs4)
+        nc.sync.dma_start(out=bather_c[:], in_=bather.rearrange("(p t) -> p t", t=PACK))
+        nc.sync.dma_start(out=bar_c[:], in_=bar.rearrange("(p t) -> p t", t=PACK))
+        w3_raw = load_weight(w3, "w3_raw")
+
+        def first_product(half, b, v_planes, w_codes, w_scales, tag):
             acc = psum.tile([P, BANK], F32, name="acc", tag=tag)
-            cols = slice(jt * P, (jt + 1) * P)
             for a in range(PASSES):
                 nc.tensor.matmul_mx(
                     out=acc[:],
-                    lhsT=v_w[a][:, cols].bitcast(FP8X4),
-                    lhsT_scale=v_s[a][:, cols],
+                    lhsT=v_w[a, half][:, b * P : (b + 1) * P].bitcast(FP8X4),
+                    lhsT_scale=v_planes[a][:, half * BANK + b * P : half * BANK + (b + 1) * P],
                     rhs=w_codes[a],
                     rhs_scale=w_scales[a],
                     start=(a == 0),
                     stop=(a == PASSES - 1),
                 )
-            return acc
+            return acc[:].rearrange("p (m t) -> p t m", t=PACK)
 
-        u = []
-        for jt in range(JT):
-            acc = first_product(
-                jt, [w1_w[:, a, :].bitcast(FP4X4) for a in range(PASSES)], [w1_s[:, a, :] for a in range(PASSES)], "bank_a"
+        w1_codes = [w1_w[:, a, :].bitcast(FP4X4) for a in range(PASSES)]
+        w1_planes = [w1_s[:, a, :] for a in range(PASSES)]
+
+        def tanh_a(half):
+            th = []
+            for b in range(BLOCKS):
+                acc = first_product(half, b, [plane[:] for plane in v_s], w1_codes, w1_planes, "bank_a")
+                if half == 0 and b == BLOCKS - 1:
+                    th.append(sb.tile([P, PACK, P], F32, name="th", tag="th_or_words", align_bytes=64))
+                else:
+                    th.append(sb.tile([P, PACK, P], F32, name="th", tag="th", bufs=BLOCKS))
+                nc.scalar.activation(th[b][:], acc, ACT.Tanh)
+            return th
+
+        th = tanh_a(0)
+
+        def quantise(raw, codes, scales):
+            width = raw.shape[2]
+            grouped = sb.tile([P, width, PACK], BF16, name="w_bf", tag="w_bf", bufs=3, align_bytes=64)
+            nc.vector.tensor_copy(
+                grouped[:].rearrange("p (c e) i -> p c i e", e=4), raw.rearrange("p i (c e) -> p c i e", e=4)
             )
-            u.append(sb.tile([P, PACK, P], F32, name="u%d" % jt, tag="u_or_out", bufs=JT))
-            nc.scalar.activation(u[jt][:], acc[:].rearrange("p (m t) -> p t m", t=PACK), ACT.Tanh)
+            nc.vector.quantize_mx(out=codes.bitcast(FP8X4), scales=scales, in_=grouped[:].rearrange("p c i -> p (c i)"))
 
         w2_codes, w2_scales = [], []
         for a in range(PASSES):
-            grouped = sb.tile([P, H, PACK], BF16, name="w2_bf%d" % a, tag="w_bf", bufs=3, align_bytes=64)
-            dst = grouped[:].rearrange("p (c e) i -> p c i e", e=4)
-            src = w2_raw[a][:].rearrange("p i (c e) -> p c i e", e=4)
-            nc.vector.tensor_copy(dst, src)
             codes = sb.tile([P, H], U32, name="w2_q%d" % a, align_bytes=64)
             scales = sb.tile([P, H], U8, name="w2_s%d" % a, align_bytes=64)
-            nc.vector.quantize_mx(
-                out=codes[:].bitcast(FP8X4), scales=scales[:], in_=grouped[:].rearrange("p c i -> p (c i)")
-            )
+            if a < PASSES - 1:
+                quantise(w2_raw[a][:], codes[:], scales[:])
+            else:
+                for c in range(2):
+                    cols = slice(c * H // 2, (c + 1) * H // 2)
+                    quantise(last_raw[c][:], codes[:, cols], scales[:, cols])
             w2_codes.append(codes[:].bitcast(FP8X4))
             w2_scales.append(scales[:])
 
-        for jt in range(JT):
-            acc = first_product(jt, w2_codes, w2_scales, "bank_b")
-            nc.vector.tensor_tensor(u[jt][:], acc[:].rearrange("p (m t) -> p t m", t=PACK), u[jt][:], ALU.mult)
+        def times_b(half, th, u):
+            for b in range(BLOCKS):
+                acc = first_product(half, b, [v_s[0][4 * a : P, :] for a in range(PASSES)], w2_codes, w2_scales, "bank_b")
+                nc.vector.tensor_tensor(u[:, b, :, :], acc, th[b][:], ALU.mult)
 
-        def make_h(t):
-            h = early[:, PACK, :] if t == PACK - 1 else sb.tile([P, S], F32, name="h%d" % t)[:]
-            for half in range(HALVES):
-                turned = psum.tile([P, 4, P], F32, name="turned", tag="bank_a")
-                for b in range(4):
-                    jt = 4 * half + b
-                    nc.tensor.transpose(turned[:, b, :], tide_sb[t][:, jt * P : (jt + 1) * P], ident[:])
-                tide_t = sb.tile([P, 4, P], F32, name="tide_t", tag="tide_t_or_gate", bufs=8)
-                nc.scalar.copy(tide_t[:], turned[:])
-                acc = psum.tile([P, 4, P], F32, name="acc_h", tag="bank_a")
-                for b in range(4):
-                    jt = 4 * half + b
-                    nc.tensor.matmul(acc[:, b, :], u[jt][:, t, :], ident[:], start=True, stop=False, is_transpose=True)
-                    nc.tensor.matmul(acc[:, b, :], tide_t[:, b, :], ident[:], start=False, stop=True, is_transpose=True)
-                nc.scalar.copy(h[:, half * BANK : (half + 1) * BANK], acc[:].rearrange("p b j -> p (b j)"))
-            return h
+        def turn_tide(t, half):
+            turned = psum.tile([P, BLOCKS, P], F32, name="turned", tag="bank_b" if half == 0 and t > 0 else "bank_a")
+            for b in range(BLOCKS):
+                nc.tensor.transpose(turned[:, b, :], tide_sb[half][:, t, b * P : (b + 1) * P], ident[:])
+            tide_t = sb.tile([P, BLOCKS, P], F32, name="tide_t", tag="tide_t_or_gate", bufs=8)
+            nc.scalar.copy(tide_t[:], turned[:])
+            return tide_t
 
-        def scatter(t):
-            h = make_h(t)
-            pieces = HALVES if t == 0 else 1
-            width = S // pieces
-            for i in range(pieces):
-                cols = slice(i * width, (i + 1) * width)
-                offsets = idx2[:, i * width // 16 : (i + 1) * width // 16]
-                nc.vector.tensor_tensor(page[t][:].indirect(offsets), h[:, cols], wgs_sb[t][:, cols], ALU.mult)
+        def scatter(t, half, u, h):
+            tide_t = turn_tide(t, half)
+            acc = psum.tile([P, BLOCKS, P], F32, name="acc_h", tag="bank_a")
+            for b in range(BLOCKS):
+                nc.tensor.matmul(acc[:, b, :], u[:, b, t, :], ident[:], start=True, stop=False, is_transpose=True)
+                nc.tensor.matmul(acc[:, b, :], tide_t[:, b, :], ident[:], start=False, stop=True, is_transpose=True)
+            nc.scalar.copy(h, acc[:].rearrange("p b j -> p (b j)"))
+            nc.vector.tensor_tensor(
+                page[t][:].indirect(half_list(idx2, half)), h, wgs_sb[t, half], ALU.mult
+            )
 
-        x = [sb.tile([P, BANK, PACK], BF16, name="x%d" % half, tag="x%d" % half, align_bytes=64) for half in range(HALVES)]
-        sandbar = [None] * PACK
-        gate = {}
-
-        def reread_bathers(t):
-            cells = reread[:, t, :]
-            for half in range(HALVES):
-                cols = slice(half * BANK, (half + 1) * BANK)
-                nc.vector.tensor_copy(cells[:, cols], page[t][:].indirect(idx3[:, half * 32 : (half + 1) * 32]))
-                nc.scalar.activation(x[half][:, :, t], cells[:, cols], ACT.Abs, scale=bather_c[:, t : t + 1])
-
-        def reread_sandbar(t):
-            if t < PACK - 1:
-                sandbar[t] = reread[:, PACK + t, :]
-            else:
-                sandbar[t] = sb.tile([P, M], F32, name="sandbar", tag="x0", align_bytes=64)[:]
-            nc.vector.tensor_copy(sandbar[t], page[t][:].indirect(idx4[:]))
-            for half in range(HALVES):
-                gate[t, half] = sb.tile([P, BANK], F32, name="gate", tag="tide_t_or_gate", bufs=8)
-                nc.scalar.activation(
-                    gate[t, half][:], sandbar[t][:, half * BANK : (half + 1) * BANK], ACT.Sigmoid, scale=bar_c[:, t : t + 1]
-                )
-
+        u = sb.tile([P, BLOCKS * H], F32, name="u0", tag="u0_or_out")[:].rearrange("p (b t m) -> p b t m", b=BLOCKS, t=PACK)
+        times_b(0, th, u)
+        gather_words(0, 1, "th_or_words")
         for t in range(PACK):
-            scatter(t)
+            h = sb.tile([P, BANK], F32, name="h", tag="u1_or_out" if t == 2 else "h%d" % t)
+            scatter(t, 0, u, h[:])
+        th = tanh_a(1)
+        u = sb.tile([P, BLOCKS * H], F32, name="u1", tag="u1_or_out")[:].rearrange("p (b t m) -> p b t m", b=BLOCKS, t=PACK)
+        times_b(1, th, u)
+        for t in range(PACK):
+            scatter(t, 1, u, early[:, (PACK + t) * BANK : (PACK + t + 1) * BANK])
 
         w3_bf = sb.tile([P, PACK, P, PACK], BF16, name="w3_bf", tag="w_bf", bufs=3, align_bytes=64)
         nc.scalar.copy(w3_bf[:].rearrange("p t m i -> p m t i"), w3_raw[:].rearrange("p i (m t) -> p m t i", t=PACK))
@@ -222,7 +240,29 @@ def tile_list_rip_lookout_board_kernel(
             out=w3_q[:].bitcast(FP8X4), scales=w3_s[:], in_=w3_bf[:].rearrange("p t m i -> p (t m i)")
         )
 
-        reread = sb.tile([P, 2 * PACK - 1, M], F32, name="reread", tag="early_or_reread")
+        x = [sb.tile([P, BANK, PACK], BF16, name="x%d" % half, tag="x%d" % half, align_bytes=64) for half in range(HALVES)]
+        reread = sb.tile([P, (2 * PACK - 1) * M], F32, name="reread", tag="early_or_reread")
+        sandbar = [None] * PACK
+        gate = {}
+
+        def reread_bathers(t):
+            for half in range(HALVES):
+                cells = reread[:, t * M + half * BANK : t * M + (half + 1) * BANK]
+                nc.vector.tensor_copy(cells, page[t][:].indirect(half_list(idx3, half)))
+                nc.scalar.activation(x[half][:, :, t], cells, ACT.Abs, scale=bather_c[:, t : t + 1])
+
+        def reread_sandbar(t):
+            if t < PACK - 1:
+                sandbar[t] = reread[:, (PACK + t) * M : (PACK + t + 1) * M]
+            else:
+                sandbar[t] = sb.tile([P, M], F32, name="sandbar", tag="x0", align_bytes=64)[:]
+            nc.vector.tensor_copy(sandbar[t], page[t][:].indirect(idx4[:]))
+            for half in range(HALVES):
+                gate[t, half] = sb.tile([P, BANK], F32, name="gate", tag="tide_t_or_gate", bufs=8)
+                nc.scalar.activation(
+                    gate[t, half][:], sandbar[t][:, half_cols(half)], ACT.Sigmoid, scale=bar_c[:, t : t + 1]
+                )
+
         for t in range(PACK):
             reread_bathers(t)
         for t in range(PACK - 1):
@@ -238,8 +278,8 @@ def tile_list_rip_lookout_board_kernel(
             )
         reread_sandbar(PACK - 1)
         for half in range(HALVES):
-            cols = slice(half * BANK, (half + 1) * BANK)
-            res = []
+            cols = half_cols(half)
+            res = sb.tile([P, PACK * BANK], F32, name="res", tag="u%d_or_out" % half)[:].rearrange("p (t m) -> p t m", t=PACK)
             for t in range(PACK):
                 y = psum.tile([P, BANK], F32, name="y", tag="bank_b")
                 nc.tensor.matmul_mx(
@@ -251,10 +291,9 @@ def tile_list_rip_lookout_board_kernel(
                     start=True,
                     stop=True,
                 )
-                res.append(sb.tile([P, BANK], F32, name="res", tag="u_or_out", bufs=JT))
-                nc.vector.tensor_tensor(res[t][:], y[:], gate[t, half][:], ALU.mult)
+                nc.vector.tensor_tensor(res[:, t, :], y[:], gate[t, half][:], ALU.mult)
                 for done in ([t - 1] if t > 0 else []) + ([t] if t == PACK - 1 else []):
                     nc.vector.scalar_tensor_tensor(
-                        res[done][:], sandbar[done][:, cols], bar_c[:, done : done + 1], res[done][:], ALU.mult, ALU.add
+                        res[:, done, :], sandbar[done][:, cols], bar_c[:, done : done + 1], res[:, done, :], ALU.mult, ALU.add
                     )
-                    nc.sync.dma_start(out=out_rows[done][:, cols], in_=res[done][:])
+                    nc.sync.dma_start(out=out_rows[done][:, cols], in_=res[:, done, :])

@@ -114,7 +114,7 @@ def tile_list_rip_lookout_board_kernel(
 
         def load_wgs(half, t0, t1):
             tile = sb.tile([P, t1 - t0, BANK], F32, name="wgs%d_%d" % (half, t0))
-            for q in range(4):
+            for q in (0, 2, 1, 3):
                 nc.sync.dma_start(out=tile[32 * q : 32 * q + 32, :, :], in_=wgs_rows[:, t0:t1, half_cols(half)])
             for t in range(t0, t1):
                 wgs_sb[t, half] = tile[:, t - t0, :]
@@ -245,11 +245,16 @@ def tile_list_rip_lookout_board_kernel(
         sandbar = [None] * PACK
         gate = {}
 
-        def reread_bathers(t):
-            for half in range(HALVES):
-                cells = reread[:, t * M + half * BANK : t * M + (half + 1) * BANK]
+        def reread_bathers(half):
+            planes = sb.tile([P, PACK * BANK], BF16, name="planes", tag="w_bf", bufs=3, align_bytes=64)
+            for t in range(PACK):
+                cells = reread[:, (half * PACK + t) * BANK : (half * PACK + t + 1) * BANK]
                 nc.vector.tensor_copy(cells, page[t][:].indirect(half_list(idx3, half)))
-                nc.scalar.activation(x[half][:, :, t], cells, ACT.Abs, scale=bather_c[:, t : t + 1])
+                nc.scalar.activation(planes[:, t * BANK : (t + 1) * BANK], cells, ACT.Abs, scale=bather_c[:, t : t + 1])
+            nc.scalar.copy(
+                x[half][:].rearrange("p (c e) t -> p c t e", e=4),
+                planes[:].rearrange("p (t c e) -> p c t e", t=PACK, e=4),
+            )
 
         def reread_sandbar(t):
             if t < PACK - 1:
@@ -263,8 +268,8 @@ def tile_list_rip_lookout_board_kernel(
                     gate[t, half][:], sandbar[t][:, half_cols(half)], ACT.Sigmoid, scale=bar_c[:, t : t + 1]
                 )
 
-        for t in range(PACK):
-            reread_bathers(t)
+        for half in range(HALVES):
+            reread_bathers(half)
         for t in range(PACK - 1):
             reread_sandbar(t)
 

@@ -19,11 +19,18 @@ ALU = mybir.AluOpType
 
 P = 128
 PACK = 4
-PASSES = K // (P * PACK)
+K_PASS = P * PACK
+PASSES = K // K_PASS
 BANK = 512
 HALVES = S // BANK
 BLOCKS = BANK // P
 LIST_COLS = BANK // 16
+TILES = H // P
+QUADRANTS = P // 32
+SCALE_ROWS = 4
+PLANE_SPAN = 32 * (QUADRANTS - 1) + SCALE_ROWS
+W2_GROUPS = ((0, 1), (1, 2), (2, 4))
+GPSIMD_SUMS = 3
 
 
 def tile_list_rip_lookout_board_kernel(
@@ -33,7 +40,7 @@ def tile_list_rip_lookout_board_kernel(
     with ExitStack() as ctx:
         lists = ctx.enter_context(tc.tile_pool(name="lists", bufs=1))
         sb = ctx.enter_context(tc.tile_pool(name="sb", bufs=1))
-        psum = ctx.enter_context(tc.psum_pool(name="psum", bufs=4))
+        psum = ctx.enter_context(tc.psum_pool(name="psum", bufs=1))
 
         idx1 = lists.tile([P, S // 16], U16, name="idx1")
         idx2 = lists.tile([P, S // 16], U16, name="idx2")
@@ -46,7 +53,7 @@ def tile_list_rip_lookout_board_kernel(
         def half_list(idx, half):
             return idx[:, half * LIST_COLS : (half + 1) * LIST_COLS]
 
-        tab_s = sb.tile([P, T], U8, name="tab_s", align_bytes=64)
+        tab_s = sb.tile([P, T], U8, name="tab_s", tag="tab_s_or_words", align_bytes=64)
         w1_s = sb.tile([P, PASSES, H], U8, name="w1_s", align_bytes=64)
         v_s = [sb.tile([P, S], U8, name="v_s%d" % a, align_bytes=64) for a in range(PASSES)]
         nc.gpsimd.memset(tab_s[:].bitcast(I32), 0)
@@ -54,36 +61,45 @@ def tile_list_rip_lookout_board_kernel(
         for a in range(1, PASSES):
             nc.vector.memset(v_s[a][:].bitcast(I32), 0)
 
-        tab_w = [sb.tile([P, T], I32, name="tab_w%d" % a, align_bytes=64) for a in range(PASSES)]
+        tab_w = [sb.tile([P, T], I32, name="tab_w", tag="tab%d" % a, align_bytes=64) for a in range(PASSES)]
         w1_w = sb.tile([P, PASSES, 2 * H], U8, name="w1_w", align_bytes=64)
 
         def load_table(a):
             nc.sync.dma_start(out=tab_w[a][:], in_=tab_words[a].rearrange("p n i -> p (n i)").bitcast(I32))
 
-        def load_weight(rows, name):
-            raw = sb.tile([P, PACK, H], F32, name=name, tag="w_raw", bufs=2)
-            nc.sync.dma_start(out=raw[:], in_=rows.rearrange("(p i) c -> p i c", i=PACK))
-            return raw
-
         nc.sync.dma_start(idx1[:], offs)
         load_table(0)
-        for q in range(4):
-            queue = nc.scalar if q < 2 else nc.sync
+        nc.sync.dma_start(idx2[:], offs2)
+        for q in range(QUADRANTS):
+            queue = nc.scalar if q < QUADRANTS // 2 else nc.sync
             queue.dma_start(
-                out=tab_s[32 * q : 32 * q + 4 * PASSES, :].bitcast(I32),
-                in_=tab_scales[:, 4 * q : 4 * q + 4, :].bitcast(I32),
+                out=tab_s[32 * q : 32 * q + SCALE_ROWS * PASSES, :].bitcast(I32),
+                in_=tab_scales[:, SCALE_ROWS * q : SCALE_ROWS * (q + 1), :].bitcast(I32),
             )
         load_table(1)
         load_table(2)
         nc.sync.dma_start(out=w1_w[:].bitcast(I32), in_=w1_words.rearrange("a p n -> p a n").bitcast(I32))
-        for q in range(4):
-            nc.sync.dma_start(
-                out=w1_s[32 * q : 32 * q + 4, :, :].bitcast(I32),
-                in_=w1_scales[:, 4 * q : 4 * q + 4, :].rearrange("a r n -> r a n").bitcast(I32),
+        for q in range(QUADRANTS):
+            nc.gpsimd.dma_start(
+                out=w1_s[32 * q : 32 * q + SCALE_ROWS, :, :].bitcast(I32),
+                in_=w1_scales[:, SCALE_ROWS * q : SCALE_ROWS * (q + 1), :].rearrange("a r n -> r a n").bitcast(I32),
             )
-        w2_raw = [load_weight(w2[512 * a : 512 * (a + 1), :], "w2_raw%d" % a) for a in range(1)]
+        w2_raw = {}
+
+        def load_w2(a, group):
+            c0, c1 = W2_GROUPS[group]
+            w2_raw[a, group] = sb.tile([P, PACK, (c1 - c0) * P], F32, name="w2_raw", tag="w2_raw", bufs=2 * PASSES)
+            rows = w2[K_PASS * a : K_PASS * (a + 1), c0 * P : c1 * P]
+            nc.sync.dma_start(out=w2_raw[a, group][:], in_=rows.rearrange("(p i) c -> p i c", i=PACK))
+
+        for a in range(PASSES):
+            load_w2(a, 0)
         ident = sb.tile([P, P], F32, name="ident")
         make_identity(nc, ident[:])
+        ident_bf = sb.tile([P, P], BF16, name="ident_bf")
+        make_identity(nc, ident_bf[:])
+        vectors = sb.tile([P, P], F32, name="vectors")
+        nc.gpsimd.memset(vectors[:], 0.0)
 
         v_w = {}
 
@@ -93,212 +109,243 @@ def tile_list_rip_lookout_board_kernel(
 
         gather_words(0, 0, "v_w00")
         nc.vector.tensor_copy(v_s[0][:], tab_s[:].indirect(idx1[:]))
+        gather_words(0, 1, "tab_s_or_words")
         for a in range(1, PASSES):
             for half in range(HALVES):
                 gather_words(a, half, "v_w%d%d" % (a, half))
         for a in range(1, PASSES):
-            nc.sync.dma_start(out=v_s[a][0:100, :].bitcast(I32), in_=v_s[0][4 * a : 4 * a + 100, :].bitcast(I32))
-
-        tide_rows = tide.rearrange("(p t) j -> p t j", t=PACK)
-        page_rows = page0.rearrange("(p t) c -> t p c", t=PACK)
-        wgs_rows = wgs.rearrange("(i t) j -> i t j", t=PACK)
-        page = [sb.tile([P, T2], F32, name="page%d" % t) for t in range(PACK)]
-        tide_sb, wgs_sb = {}, {}
-
-        def load_tide(half, tile):
-            tide_sb[half] = tile.rearrange("p (t j) -> p t j", t=PACK)
-            nc.sync.dma_start(out=tide_sb[half], in_=tide_rows[:, :, half_cols(half)])
-
-        def load_page(t):
-            nc.sync.dma_start(out=page[t][:], in_=page_rows[t])
-
-        def load_wgs(half, t0, t1):
-            tile = sb.tile([P, t1 - t0, BANK], F32, name="wgs%d_%d" % (half, t0))
-            for q in (0, 2, 1, 3):
-                nc.sync.dma_start(out=tile[32 * q : 32 * q + 32, :, :], in_=wgs_rows[:, t0:t1, half_cols(half)])
-            for t in range(t0, t1):
-                wgs_sb[t, half] = tile[:, t - t0, :]
-
-        w2_raw.append(load_weight(w2[512:1024, :], "w2_raw1"))
-        last_raw = []
-        for c in range(2):
-            last_raw.append(sb.tile([P, PACK, H // 2], F32, name="w2_last%d" % c))
             nc.sync.dma_start(
-                out=last_raw[c][:], in_=w2[1024:1536, c * H // 2 : (c + 1) * H // 2].rearrange("(p i) c -> p i c", i=PACK)
+                out=v_s[a][0:PLANE_SPAN, :].bitcast(I32),
+                in_=v_s[0][SCALE_ROWS * a : SCALE_ROWS * a + PLANE_SPAN, :].bitcast(I32),
             )
-        load_tide(0, sb.tile([P, PACK * BANK], F32, name="tide_first")[:])
-        nc.sync.dma_start(idx2[:], offs2)
+
+        page = [sb.tile([P, T2], F32, name="page%d" % c) for c in range(TILES)]
+        tide_sb = sb.tile([P, TILES * S], F32, name="tide_sb", tag="tide_or_gate")
+        wgs_sb = sb.tile([P, S], F32, name="wgs_sb")
+
+        def load_tide(c, cols):
+            nc.sync.dma_start(out=tide_sb[:, c * S + cols.start : c * S + cols.stop], in_=tide[c * P : (c + 1) * P, cols])
+
+        def load_page(c):
+            nc.sync.dma_start(out=page[c][:], in_=page0[c * P : (c + 1) * P, :])
+
+        def load_wgs(half):
+            nc.sync.dma_start(out=wgs_sb[:, half_cols(half)], in_=wgs[:, half_cols(half)])
+
         load_page(0)
-        load_wgs(0, 0, 2)
-        load_page(1)
-        load_wgs(0, 2, 4)
-        load_page(2)
-        load_page(3)
-        early = sb.tile([P, 2 * PACK * BANK], F32, name="early", tag="early_or_reread")
-        load_tide(1, early[:, 0 : PACK * BANK])
-        load_wgs(1, 0, 4)
-        bather_c = sb.tile([P, PACK], F32, name="bather_c")
-        bar_c = sb.tile([P, PACK], F32, name="bar_c")
+        load_tide(0, half_cols(0))
+        load_wgs(0)
+        for a in range(PASSES):
+            load_w2(a, 1)
+        load_tide(0, half_cols(1))
+        load_wgs(1)
+        load_tide(1, slice(0, S))
+        for a in range(PASSES):
+            load_w2(a, 2)
+        for c in range(2, TILES):
+            load_tide(c, slice(0, S))
+        for c in range(1, TILES):
+            load_page(c)
         nc.sync.dma_start(idx3[:], offs3)
         nc.sync.dma_start(idx4[:], offs4)
-        nc.sync.dma_start(out=bather_c[:], in_=bather.rearrange("(p t) -> p t", t=PACK))
-        nc.sync.dma_start(out=bar_c[:], in_=bar.rearrange("(p t) -> p t", t=PACK))
-        w3_raw = load_weight(w3, "w3_raw")
+        nc.sync.dma_start(out=vectors[0:TILES, :], in_=bather.rearrange("(c p) -> c p", p=P))
+        nc.sync.dma_start(out=vectors[TILES : 2 * TILES, :], in_=bar.rearrange("(c p) -> c p", p=P))
+        w3_raw = sb.tile([P, PACK, H], F32, name="w3_raw", tag="tab2", align_bytes=64)
+        nc.sync.dma_start(out=w3_raw[:], in_=w3.rearrange("(p i) c -> p i c", i=PACK))
 
-        def first_product(half, b, v_planes, w_codes, w_scales, tag):
-            acc = psum.tile([P, BANK], F32, name="acc", tag=tag)
+        def quantise(raw, name, copy, tag):
+            width = raw.shape[2]
+            grouped = sb.tile([P, width, PACK], BF16, name="grouped", tag=tag, align_bytes=64)
+            copy(grouped[:].rearrange("p (n e) i -> p n i e", e=4), raw.rearrange("p i (n e) -> p n i e", e=4))
+            codes = sb.tile([P, width], U32, name=name + "_codes", align_bytes=64)
+            scales = sb.tile([P, width], U8, name=name + "_scales", align_bytes=64)
+            nc.vector.quantize_mx(
+                out=codes[:].bitcast(FP8X4), scales=scales[:], in_=grouped[:].rearrange("p n i -> p (n i)")
+            )
+            return codes, scales
+
+        def quantise_w2(group):
+            return [
+                quantise(
+                    w2_raw[a, group][:],
+                    "w2_%d%d" % (a, group),
+                    nc.vector.tensor_copy if (a, group) == (PASSES - 1, 0) else nc.scalar.copy,
+                    "bf%d" % a,
+                )
+                for a in range(PASSES)
+            ]
+
+        def first_product(half, w_codes, w_scales, v_planes, bank):
+            acc = psum.tile([P, BANK], F32, name="acc", tag="bank%d" % bank)
             for a in range(PASSES):
                 nc.tensor.matmul_mx(
                     out=acc[:],
-                    lhsT=v_w[a, half][:, b * P : (b + 1) * P].bitcast(FP8X4),
-                    lhsT_scale=v_planes[a][:, half * BANK + b * P : half * BANK + (b + 1) * P],
-                    rhs=w_codes[a],
-                    rhs_scale=w_scales[a],
+                    lhsT=w_codes[a],
+                    lhsT_scale=w_scales[a],
+                    rhs=v_w[a, half][:].bitcast(FP8X4),
+                    rhs_scale=v_planes[a][:, half_cols(half)],
                     start=(a == 0),
                     stop=(a == PASSES - 1),
                 )
-            return acc[:].rearrange("p (m t) -> p t m", t=PACK)
+            return acc
 
-        w1_codes = [w1_w[:, a, :].bitcast(FP4X4) for a in range(PASSES)]
-        w1_planes = [w1_s[:, a, :] for a in range(PASSES)]
+        def gated_product(c, group, w2_q, u):
+            first_tile = W2_GROUPS[group][0]
+            cols = slice((c - first_tile) * P, (c - first_tile + 1) * P)
+            for half in range(HALVES):
+                acc_a = first_product(
+                    half,
+                    [w1_w[:, a, 2 * c * P : 2 * (c + 1) * P].bitcast(FP4X4) for a in range(PASSES)],
+                    [w1_s[:, a, c * P : (c + 1) * P] for a in range(PASSES)],
+                    [plane[:] for plane in v_s],
+                    half,
+                )
+                th = sb.tile([P, BANK], F32, name="th", tag="th_or_sand", bufs=TILES * HALVES)
+                nc.scalar.activation(th[:], acc_a[:], ACT.Tanh)
+                acc_b = first_product(
+                    half,
+                    [codes[:, cols].bitcast(FP8X4) for codes, scales in w2_q],
+                    [scales[:, cols] for codes, scales in w2_q],
+                    [v_s[0][SCALE_ROWS * a : P, :] for a in range(PASSES)],
+                    2 + 2 * (c % 2) + half,
+                )
+                nc.vector.tensor_tensor(u[half], acc_b[:], th[:], ALU.mult)
 
-        def tanh_a(half):
-            th = []
-            for b in range(BLOCKS):
-                acc = first_product(half, b, [plane[:] for plane in v_s], w1_codes, w1_planes, "bank_a")
-                if half == 0 and b == BLOCKS - 1:
-                    th.append(sb.tile([P, PACK, P], F32, name="th", tag="th_or_words", align_bytes=64))
-                else:
-                    th.append(sb.tile([P, PACK, P], F32, name="th", tag="th", bufs=BLOCKS))
-                nc.scalar.activation(th[b][:], acc, ACT.Tanh)
-            return th
+        def add_tide_by_transposes(c, u, h):
+            for half in range(HALVES):
+                summed = psum.tile([P, BLOCKS, P], F32, name="summed", tag="bank%d" % (6 + half))
+                for b in range(BLOCKS):
+                    j0 = half * BANK + b * P
+                    nc.tensor.matmul(summed[:, b, :], u[:, j0 : j0 + P], ident[:], start=True, stop=False, is_transpose=True)
+                    nc.tensor.matmul(
+                        summed[:, b, :],
+                        tide_sb[:, c * S + j0 : c * S + j0 + P],
+                        ident[:],
+                        start=False,
+                        stop=True,
+                        is_transpose=True,
+                    )
+                by_entry = sb.tile([P, BLOCKS, P], F32, name="by_entry", tag="by_entry", bufs=HALVES)
+                nc.scalar.copy(by_entry[:], summed[:])
+                by_row = psum.tile([P, BLOCKS, P], F32, name="by_row", tag="bank%d" % half)
+                for b in range(BLOCKS):
+                    nc.tensor.transpose(by_row[:, b, :], by_entry[:, b, :], ident[:])
+                nc.scalar.copy(h[:, half_cols(half)], by_row[:].rearrange("p b j -> p (b j)"))
 
-        th = tanh_a(0)
+        h0 = [sb.tile([P, BANK], F32, name="h0", tag="out%d" % half)[:] for half in range(HALVES)]
+        gated_product(0, 0, quantise_w2(0), h0)
+        nc.vector.tensor_tensor(h0[0], h0[0], tide_sb[:, half_cols(0)], ALU.add)
+        nc.vector.tensor_tensor(page[0][:].indirect(half_list(idx2, 0)), h0[0], wgs_sb[:, half_cols(0)], ALU.mult)
+        w2_q = quantise_w2(1)
+        nc.vector.tensor_tensor(h0[1], h0[1], tide_sb[:, half_cols(1)], ALU.add)
+        nc.vector.tensor_tensor(page[0][:].indirect(half_list(idx2, 1)), h0[1], wgs_sb[:, half_cols(1)], ALU.mult)
+        u1 = sb.tile([P, S], F32, name="u1", tag="tab1", align_bytes=64)
+        gated_product(1, 1, w2_q, [u1[:, half_cols(half)] for half in range(HALVES)])
+        w2_q = quantise_w2(2)
+        h1 = sb.tile([P, S], F32, name="h1", tag="bf%d" % (PASSES - 1), align_bytes=64)
+        nc.vector.tensor_tensor(h1[:], u1[:], tide_sb[:, S : 2 * S], ALU.add)
+        u23 = sb.tile([P, 2 * S], F32, name="u23", tag="tab0", align_bytes=64)
+        h23 = sb.tile([P, 2 * S], F32, name="h23", tag="h_or_reread")
+        u_late = {c: u23[:, (c - 2) * S : (c - 1) * S] for c in range(2, TILES)}
+        h_late = {c: h23[:, (c - 2) * S : (c - 1) * S] for c in range(2, TILES)}
+        for c in range(2, TILES):
+            gated_product(c, 2, w2_q, [u_late[c][:, half_cols(half)] for half in range(HALVES)])
+        for c in range(2, TILES):
+            add_tide_by_transposes(c, u_late[c], h_late[c])
+        nc.vector.tensor_tensor(page[1][:].indirect(idx2[:]), h1[:], wgs_sb[:], ALU.mult)
+        for c in range(2, TILES):
+            nc.vector.tensor_tensor(page[c][:].indirect(idx2[:]), h_late[c], wgs_sb[:], ALU.mult)
 
-        def quantise(raw, codes, scales):
-            width = raw.shape[2]
-            grouped = sb.tile([P, width, PACK], BF16, name="w_bf", tag="w_bf", bufs=3, align_bytes=64)
-            nc.vector.tensor_copy(
-                grouped[:].rearrange("p (c e) i -> p c i e", e=4), raw.rearrange("p i (c e) -> p c i e", e=4)
-            )
-            nc.vector.quantize_mx(out=codes.bitcast(FP8X4), scales=scales, in_=grouped[:].rearrange("p c i -> p (c i)"))
+        turned = psum.tile([P, P], F32, name="turned", tag="bank6")
+        nc.tensor.transpose(turned[:], vectors[:], ident[:])
+        factors = sb.tile([P, 2 * TILES], F32, name="factors")
+        nc.scalar.copy(factors[:], turned[:, 0 : 2 * TILES])
+        w3_codes, w3_scales = quantise(w3_raw[:], "w3", nc.scalar.copy, "bf0")
 
-        w2_codes, w2_scales = [], []
-        for a in range(PASSES):
-            codes = sb.tile([P, H], U32, name="w2_q%d" % a, align_bytes=64)
-            scales = sb.tile([P, H], U8, name="w2_s%d" % a, align_bytes=64)
-            if a < PASSES - 1:
-                quantise(w2_raw[a][:], codes[:], scales[:])
-            else:
-                for c in range(2):
-                    cols = slice(c * H // 2, (c + 1) * H // 2)
-                    quantise(last_raw[c][:], codes[:, cols], scales[:, cols])
-            w2_codes.append(codes[:].bitcast(FP8X4))
-            w2_scales.append(scales[:])
+        def bar_of(c):
+            return factors[:, TILES + c : TILES + c + 1]
 
-        def times_b(half, th, u):
-            for b in range(BLOCKS):
-                acc = first_product(half, b, [v_s[0][4 * a : P, :] for a in range(PASSES)], w2_codes, w2_scales, "bank_b")
-                nc.vector.tensor_tensor(u[:, b, :, :], acc, th[b][:], ALU.mult)
-
-        def turn_tide(t, half):
-            turned = psum.tile([P, BLOCKS, P], F32, name="turned", tag="bank_b" if half == 0 and t > 0 else "bank_a")
-            for b in range(BLOCKS):
-                nc.tensor.transpose(turned[:, b, :], tide_sb[half][:, t, b * P : (b + 1) * P], ident[:])
-            tide_t = sb.tile([P, BLOCKS, P], F32, name="tide_t", tag="tide_t_or_gate", bufs=8)
-            nc.scalar.copy(tide_t[:], turned[:])
-            return tide_t
-
-        def scatter(t, half, u, h):
-            tide_t = turn_tide(t, half)
-            acc = psum.tile([P, BLOCKS, P], F32, name="acc_h", tag="bank_a")
-            for b in range(BLOCKS):
-                nc.tensor.matmul(acc[:, b, :], u[:, b, t, :], ident[:], start=True, stop=False, is_transpose=True)
-                nc.tensor.matmul(acc[:, b, :], tide_t[:, b, :], ident[:], start=False, stop=True, is_transpose=True)
-            nc.scalar.copy(h, acc[:].rearrange("p b j -> p (b j)"))
-            nc.vector.tensor_tensor(
-                page[t][:].indirect(half_list(idx2, half)), h, wgs_sb[t, half], ALU.mult
-            )
-
-        u = sb.tile([P, BLOCKS * H], F32, name="u0", tag="u0_or_out")[:].rearrange("p (b t m) -> p b t m", b=BLOCKS, t=PACK)
-        times_b(0, th, u)
-        gather_words(0, 1, "th_or_words")
-        for t in range(PACK):
-            h = sb.tile([P, BANK], F32, name="h", tag="u1_or_out" if t == 2 else "h%d" % t)
-            scatter(t, 0, u, h[:])
-        th = tanh_a(1)
-        u = sb.tile([P, BLOCKS * H], F32, name="u1", tag="u1_or_out")[:].rearrange("p (b t m) -> p b t m", b=BLOCKS, t=PACK)
-        times_b(1, th, u)
-        for t in range(PACK):
-            scatter(t, 1, u, early[:, (PACK + t) * BANK : (PACK + t + 1) * BANK])
-
-        w3_bf = sb.tile([P, PACK, P, PACK], BF16, name="w3_bf", tag="w_bf", bufs=3, align_bytes=64)
-        nc.scalar.copy(w3_bf[:].rearrange("p t m i -> p m t i"), w3_raw[:].rearrange("p i (m t) -> p m t i", t=PACK))
-        w3_q = sb.tile([P, H], U32, name="w3_q", align_bytes=64)
-        w3_s = sb.tile([P, H], U8, name="w3_s", align_bytes=64)
-        nc.vector.quantize_mx(
-            out=w3_q[:].bitcast(FP8X4), scales=w3_s[:], in_=w3_bf[:].rearrange("p t m i -> p (t m i)")
-        )
-
-        x = [sb.tile([P, BANK, PACK], BF16, name="x%d" % half, tag="x%d" % half, align_bytes=64) for half in range(HALVES)]
-        reread = sb.tile([P, (2 * PACK - 1) * M], F32, name="reread", tag="early_or_reread")
-        sandbar = [None] * PACK
-        gate = {}
+        x = [sb.tile([P, BANK, PACK], BF16, name="x", tag="x%d" % half, align_bytes=64) for half in range(HALVES)]
+        reread = sb.tile([P, (2 * TILES - 1) * M], F32, name="reread", tag="h_or_reread")
+        sandbar = {}
 
         def reread_bathers(half):
-            planes = sb.tile([P, PACK * BANK], BF16, name="planes", tag="w_bf", bufs=3, align_bytes=64)
-            for t in range(PACK):
-                cells = reread[:, (half * PACK + t) * BANK : (half * PACK + t + 1) * BANK]
-                nc.vector.tensor_copy(cells, page[t][:].indirect(half_list(idx3, half)))
-                nc.scalar.activation(planes[:, t * BANK : (t + 1) * BANK], cells, ACT.Abs, scale=bather_c[:, t : t + 1])
-            nc.scalar.copy(
-                x[half][:].rearrange("p (c e) t -> p c t e", e=4),
-                planes[:].rearrange("p (t c e) -> p c t e", t=PACK, e=4),
-            )
-
-        def reread_sandbar(t):
-            if t < PACK - 1:
-                sandbar[t] = reread[:, (PACK + t) * M : (PACK + t + 1) * M]
-            else:
-                sandbar[t] = sb.tile([P, M], F32, name="sandbar", tag="x0", align_bytes=64)[:]
-            nc.vector.tensor_copy(sandbar[t], page[t][:].indirect(idx4[:]))
-            for half in range(HALVES):
-                gate[t, half] = sb.tile([P, BANK], F32, name="gate", tag="tide_t_or_gate", bufs=8)
-                nc.scalar.activation(
-                    gate[t, half][:], sandbar[t][:, half_cols(half)], ACT.Sigmoid, scale=bar_c[:, t : t + 1]
+            by_cell = [
+                psum.tile([P, H], BF16, name="by_cell", tag="bank%d" % (BLOCKS * half + b)) for b in range(BLOCKS)
+            ]
+            for c in range(TILES):
+                cells = reread[:, (half * TILES + c) * BANK : (half * TILES + c + 1) * BANK]
+                nc.vector.tensor_copy(cells, page[c][:].indirect(half_list(idx3, half)))
+                rounded = sb.tile([P, BANK], BF16, name="rounded", tag="rounded", bufs=3)
+                nc.scalar.activation(rounded[:], cells, ACT.Abs, scale=factors[:, c : c + 1])
+                for b in range(BLOCKS):
+                    nc.tensor.transpose(by_cell[b][:, c * P : (c + 1) * P], rounded[:, b * P : (b + 1) * P], ident_bf[:])
+            x_words = x[half][:].rearrange("p m i -> p (m i)").bitcast(F32)
+            for pair in range(BLOCKS // 2):
+                carried = psum.tile([P, 2, 2, P], F32, name="carried", tag="bank%d" % (2 * half + pair))
+                for e in range(2):
+                    b = 2 * pair + e
+                    if (half, b) == (HALVES - 1, BLOCKS - 1):
+                        words = sb.tile([P, 2, P], F32, name="words", tag="tide_or_gate")
+                    else:
+                        words = sb.tile([P, 2, P], F32, name="words", tag="words", bufs=BLOCKS)
+                    nc.scalar.copy(words[:], by_cell[b][:].bitcast(F32).rearrange("m (p u) -> m u p", u=2))
+                    for u in range(2):
+                        nc.tensor.transpose(carried[:, e, u, :], words[:, u, :], ident[:])
+                nc.scalar.copy(
+                    x_words[:, pair * BANK : (pair + 1) * BANK].rearrange("p (e m u) -> p e m u", e=2, u=2),
+                    carried[:].rearrange("p e u m -> p e m u"),
                 )
+
+        def reread_sandbar(c, cells):
+            sandbar[c] = cells
+            nc.vector.tensor_copy(cells, page[c][:].indirect(idx4[:]))
 
         for half in range(HALVES):
             reread_bathers(half)
-        for t in range(PACK - 1):
-            reread_sandbar(t)
+        for c in range(TILES - 1):
+            reread_sandbar(c, reread[:, (TILES + c) * M : (TILES + c + 1) * M])
 
-        out_rows = out.rearrange("(p t) m -> t p m", t=PACK)
         x_q, x_s = [], []
         for half in range(HALVES):
             x_q.append(sb.tile([P, BANK], U32, name="x_q%d" % half, align_bytes=64))
             x_s.append(sb.tile([P, BANK], U8, name="x_s%d" % half, align_bytes=64))
             nc.vector.quantize_mx(
-                out=x_q[half][:].bitcast(FP8X4), scales=x_s[half][:], in_=x[half][:].rearrange("p m t -> p (m t)")
+                out=x_q[half][:].bitcast(FP8X4), scales=x_s[half][:], in_=x[half][:].rearrange("p m i -> p (m i)")
             )
-        reread_sandbar(PACK - 1)
-        for half in range(HALVES):
-            cols = half_cols(half)
-            res = sb.tile([P, PACK * BANK], F32, name="res", tag="u%d_or_out" % half)[:].rearrange("p (t m) -> p t m", t=PACK)
-            for t in range(PACK):
-                y = psum.tile([P, BANK], F32, name="y", tag="bank_b")
-                nc.tensor.matmul_mx(
-                    out=y[:],
-                    lhsT=w3_q[:, t * P : (t + 1) * P].bitcast(FP8X4),
-                    lhsT_scale=w3_s[:, t * P : (t + 1) * P],
-                    rhs=x_q[half][:].bitcast(FP8X4),
-                    rhs_scale=x_s[half][:],
-                    start=True,
-                    stop=True,
-                )
-                nc.vector.tensor_tensor(res[:, t, :], y[:], gate[t, half][:], ALU.mult)
-                for done in ([t - 1] if t > 0 else []) + ([t] if t == PACK - 1 else []):
-                    nc.vector.scalar_tensor_tensor(
-                        res[:, done, :], sandbar[done][:, cols], bar_c[:, done : done + 1], res[:, done, :], ALU.mult, ALU.add
-                    )
-                    nc.sync.dma_start(out=out_rows[done][:, cols], in_=res[:, done, :])
+        reread_sandbar(TILES - 1, sb.tile([P, M], F32, name="sandbar_last", tag="x0", align_bytes=64)[:])
+
+        gates = sb.tile([P, TILES * M], F32, name="gates", tag="tide_or_gate")
+        pieces = [(c, half) for half in range(HALVES) for c in range(TILES)]
+        gate, sand = {}, {}
+        for c, half in pieces:
+            gate[c, half] = gates[:, (half * TILES + c) * BANK : (half * TILES + c + 1) * BANK]
+            nc.scalar.activation(gate[c, half], sandbar[c][:, half_cols(half)], ACT.Sigmoid, scale=bar_of(c))
+        for c, half in pieces[:GPSIMD_SUMS]:
+            sand[c, half] = sb.tile([P, BANK], F32, name="sand", tag="th_or_sand", bufs=TILES * HALVES)
+            nc.scalar.activation(sand[c, half][:], sandbar[c][:, half_cols(half)], ACT.Copy, scale=bar_of(c))
+        res = [sb.tile([P, TILES * BANK], F32, name="res", tag="out%d" % half) for half in range(HALVES)]
+        for c, half in pieces:
+            y = psum.tile([P, BANK], F32, name="y", tag="bank%d" % (TILES * (1 - half) + c))
+            nc.tensor.matmul_mx(
+                out=y[:],
+                lhsT=w3_codes[:, c * P : (c + 1) * P].bitcast(FP8X4),
+                lhsT_scale=w3_scales[:, c * P : (c + 1) * P],
+                rhs=x_q[half][:].bitcast(FP8X4),
+                rhs_scale=x_s[half][:],
+                start=True,
+                stop=True,
+            )
+            nc.vector.tensor_tensor(res[half][:, c * BANK : (c + 1) * BANK], y[:], gate[c, half], ALU.mult)
+        for c, half in pieces[:GPSIMD_SUMS]:
+            gated = res[half][:, c * BANK : (c + 1) * BANK]
+            nc.gpsimd.tensor_tensor(gated, gated, sand[c, half][:], ALU.add)
+            nc.sync.dma_start(out=out[c * P : (c + 1) * P, half_cols(half)], in_=gated)
+        for c, half in pieces[GPSIMD_SUMS:]:
+            parts = 2 if (c, half) == pieces[-1] else 1
+            width = BANK // parts
+            for m0 in range(0, BANK, width):
+                gated = res[half][:, c * BANK + m0 : c * BANK + m0 + width]
+                cols = slice(half * BANK + m0, half * BANK + m0 + width)
+                nc.vector.scalar_tensor_tensor(gated, sandbar[c][:, cols], bar_of(c), gated, ALU.mult, ALU.add)
+                nc.sync.dma_start(out=out[c * P : (c + 1) * P, cols], in_=gated)

from contextlib import ExitStack

import concourse.mybir as mybir
from concourse.masks import make_identity

K, H, T, S, T2, M = 1536, 512, 2048, 1024, 2048, 1024
FLOPS = 2 * (2 * K * H * S) + 2 * H * H * M

F32 = mybir.dt.float32
BF16 = mybir.dt.bfloat16
I32 = mybir.dt.int32
U32 = mybir.dt.uint32
U16 = mybir.dt.uint16
U8 = mybir.dt.uint8
FP8X4 = mybir.dt.float8_e4m3fn_x4
FP4X4 = mybir.dt.float4_e2m1fn_x4
ACT = mybir.ActivationFunctionType
ALU = mybir.AluOpType

P = 128
PACK = 4
K_PASS = P * PACK
PASSES = K // K_PASS
BANK = 512
HALVES = S // BANK
BLOCKS = BANK // P
LIST_COLS = BANK // 16
TILES = H // P
QUADRANTS = P // 32
SCALE_ROWS = 4
PLANE_SPAN = 32 * (QUADRANTS - 1) + SCALE_ROWS
W2_GROUPS = ((0, 1), (1, 2), (2, 4))
GPSIMD_SUMS = 3


def tile_list_rip_lookout_board_kernel(
    tc, tab_words, tab_scales, offs, offs2, offs3, offs4, w1_words, w1_scales, w2, tide, page0, wgs, bather, w3, bar, out
):
    nc = tc.nc
    with ExitStack() as ctx:
        lists = ctx.enter_context(tc.tile_pool(name="lists", bufs=1))
        sb = ctx.enter_context(tc.tile_pool(name="sb", bufs=1))
        psum = ctx.enter_context(tc.psum_pool(name="psum", bufs=1))

        idx1 = lists.tile([P, S // 16], U16, name="idx1")
        idx2 = lists.tile([P, S // 16], U16, name="idx2")
        idx3 = lists.tile([P, M // 16], U16, name="idx3")
        idx4 = lists.tile([P, M // 16], U16, name="idx4")

        def half_cols(half):
            return slice(half * BANK, (half + 1) * BANK)

        def half_list(idx, half):
            return idx[:, half * LIST_COLS : (half + 1) * LIST_COLS]

        tab_s = sb.tile([P, T], U8, name="tab_s", tag="tab_s_or_words", align_bytes=64)
        w1_s = sb.tile([P, PASSES, H], U8, name="w1_s", align_bytes=64)
        v_s = [sb.tile([P, S], U8, name="v_s%d" % a, align_bytes=64) for a in range(PASSES)]
        nc.gpsimd.memset(tab_s[:].bitcast(I32), 0)
        nc.gpsimd.memset(w1_s[:].bitcast(I32), 0)
        for a in range(1, PASSES):
            nc.vector.memset(v_s[a][:].bitcast(I32), 0)

        tab_w = [sb.tile([P, T], I32, name="tab_w", tag="tab%d" % a, align_bytes=64) for a in range(PASSES)]
        w1_w = sb.tile([P, PASSES, 2 * H], U8, name="w1_w", align_bytes=64)

        def load_table(a):
            nc.sync.dma_start(out=tab_w[a][:], in_=tab_words[a].rearrange("p n i -> p (n i)").bitcast(I32))

        nc.sync.dma_start(idx1[:], offs)
        load_table(0)
        nc.sync.dma_start(idx2[:], offs2)
        for q in range(QUADRANTS):
            queue = nc.scalar if q < QUADRANTS // 2 else nc.sync
            queue.dma_start(
                out=tab_s[32 * q : 32 * q + SCALE_ROWS * PASSES, :].bitcast(I32),
                in_=tab_scales[:, SCALE_ROWS * q : SCALE_ROWS * (q + 1), :].bitcast(I32),
            )
        load_table(1)
        load_table(2)
        nc.sync.dma_start(out=w1_w[:].bitcast(I32), in_=w1_words.rearrange("a p n -> p a n").bitcast(I32))
        for q in range(QUADRANTS):
            nc.gpsimd.dma_start(
                out=w1_s[32 * q : 32 * q + SCALE_ROWS, :, :].bitcast(I32),
                in_=w1_scales[:, SCALE_ROWS * q : SCALE_ROWS * (q + 1), :].rearrange("a r n -> r a n").bitcast(I32),
            )
        w2_raw = {}

        def load_w2(a, group):
            c0, c1 = W2_GROUPS[group]
            w2_raw[a, group] = sb.tile([P, PACK, (c1 - c0) * P], F32, name="w2_raw", tag="w2_raw", bufs=2 * PASSES)
            rows = w2[K_PASS * a : K_PASS * (a + 1), c0 * P : c1 * P]
            nc.sync.dma_start(out=w2_raw[a, group][:], in_=rows.rearrange("(p i) c -> p i c", i=PACK))

        for a in range(PASSES):
            load_w2(a, 0)
        ident = sb.tile([P, P], F32, name="ident")
        make_identity(nc, ident[:])
        ident_bf = sb.tile([P, P], BF16, name="ident_bf")
        make_identity(nc, ident_bf[:])
        vectors = sb.tile([P, P], F32, name="vectors")
        nc.gpsimd.memset(vectors[:], 0.0)

        v_w = {}

        def gather_words(a, half, tag):
            v_w[a, half] = sb.tile([P, BANK], U32, name="v_w", tag=tag, align_bytes=64)
            nc.vector.tensor_copy(v_w[a, half][:], tab_w[a][:].bitcast(U32).indirect(half_list(idx1, half)))

        gather_words(0, 0, "v_w00")
        nc.vector.tensor_copy(v_s[0][:], tab_s[:].indirect(idx1[:]))
        gather_words(0, 1, "tab_s_or_words")
        for a in range(1, PASSES):
            for half in range(HALVES):
                gather_words(a, half, "v_w%d%d" % (a, half))
        for a in range(1, PASSES):
            nc.sync.dma_start(
                out=v_s[a][0:PLANE_SPAN, :].bitcast(I32),
                in_=v_s[0][SCALE_ROWS * a : SCALE_ROWS * a + PLANE_SPAN, :].bitcast(I32),
            )

        page = [sb.tile([P, T2], F32, name="page%d" % c) for c in range(TILES)]
        tide_sb = sb.tile([P, TILES * S], F32, name="tide_sb", tag="tide_or_gate")
        wgs_sb = sb.tile([P, S], F32, name="wgs_sb")

        def load_tide(c, cols):
            nc.sync.dma_start(out=tide_sb[:, c * S + cols.start : c * S + cols.stop], in_=tide[c * P : (c + 1) * P, cols])

        def load_page(c):
            nc.sync.dma_start(out=page[c][:], in_=page0[c * P : (c + 1) * P, :])

        def load_wgs(half):
            nc.sync.dma_start(out=wgs_sb[:, half_cols(half)], in_=wgs[:, half_cols(half)])

        load_page(0)
        load_tide(0, half_cols(0))
        load_wgs(0)
        for a in range(PASSES):
            load_w2(a, 1)
        load_tide(0, half_cols(1))
        load_wgs(1)
        load_tide(1, slice(0, S))
        for a in range(PASSES):
            load_w2(a, 2)
        for c in range(2, TILES):
            load_tide(c, slice(0, S))
        for c in range(1, TILES):
            load_page(c)
        nc.sync.dma_start(idx3[:], offs3)
        nc.sync.dma_start(idx4[:], offs4)
        nc.sync.dma_start(out=vectors[0:TILES, :], in_=bather.rearrange("(c p) -> c p", p=P))
        nc.sync.dma_start(out=vectors[TILES : 2 * TILES, :], in_=bar.rearrange("(c p) -> c p", p=P))
        w3_raw = sb.tile([P, PACK, H], F32, name="w3_raw", tag="tab2", align_bytes=64)
        nc.sync.dma_start(out=w3_raw[:], in_=w3.rearrange("(p i) c -> p i c", i=PACK))

        def quantise(raw, name, copy, tag):
            width = raw.shape[2]
            grouped = sb.tile([P, width, PACK], BF16, name="grouped", tag=tag, align_bytes=64)
            copy(grouped[:].rearrange("p (n e) i -> p n i e", e=4), raw.rearrange("p i (n e) -> p n i e", e=4))
            codes = sb.tile([P, width], U32, name=name + "_codes", align_bytes=64)
            scales = sb.tile([P, width], U8, name=name + "_scales", align_bytes=64)
            nc.vector.quantize_mx(
                out=codes[:].bitcast(FP8X4), scales=scales[:], in_=grouped[:].rearrange("p n i -> p (n i)")
            )
            return codes, scales

        def quantise_w2(group):
            return [
                quantise(
                    w2_raw[a, group][:],
                    "w2_%d%d" % (a, group),
                    nc.vector.tensor_copy if (a, group) == (PASSES - 1, 0) else nc.scalar.copy,
                    "bf%d" % a,
                )
                for a in range(PASSES)
            ]

        def first_product(half, w_codes, w_scales, v_planes, bank):
            acc = psum.tile([P, BANK], F32, name="acc", tag="bank%d" % bank)
            for a in range(PASSES):
                nc.tensor.matmul_mx(
                    out=acc[:],
                    lhsT=w_codes[a],
                    lhsT_scale=w_scales[a],
                    rhs=v_w[a, half][:].bitcast(FP8X4),
                    rhs_scale=v_planes[a][:, half_cols(half)],
                    start=(a == 0),
                    stop=(a == PASSES - 1),
                )
            return acc

        def gated_product(c, group, w2_q, u):
            first_tile = W2_GROUPS[group][0]
            cols = slice((c - first_tile) * P, (c - first_tile + 1) * P)
            for half in range(HALVES):
                acc_a = first_product(
                    half,
                    [w1_w[:, a, 2 * c * P : 2 * (c + 1) * P].bitcast(FP4X4) for a in range(PASSES)],
                    [w1_s[:, a, c * P : (c + 1) * P] for a in range(PASSES)],
                    [plane[:] for plane in v_s],
                    half,
                )
                th = sb.tile([P, BANK], F32, name="th", tag="th_or_sand", bufs=TILES * HALVES)
                nc.scalar.activation(th[:], acc_a[:], ACT.Tanh)
                acc_b = first_product(
                    half,
                    [codes[:, cols].bitcast(FP8X4) for codes, scales in w2_q],
                    [scales[:, cols] for codes, scales in w2_q],
                    [v_s[0][SCALE_ROWS * a : P, :] for a in range(PASSES)],
                    2 + 2 * (c % 2) + half,
                )
                nc.vector.tensor_tensor(u[half], acc_b[:], th[:], ALU.mult)

        def add_tide_by_transposes(c, u, h):
            for half in range(HALVES):
                summed = psum.tile([P, BLOCKS, P], F32, name="summed", tag="bank%d" % (6 + half))
                for b in range(BLOCKS):
                    j0 = half * BANK + b * P
                    nc.tensor.matmul(summed[:, b, :], u[:, j0 : j0 + P], ident[:], start=True, stop=False, is_transpose=True)
                    nc.tensor.matmul(
                        summed[:, b, :],
                        tide_sb[:, c * S + j0 : c * S + j0 + P],
                        ident[:],
                        start=False,
                        stop=True,
                        is_transpose=True,
                    )
                by_entry = sb.tile([P, BLOCKS, P], F32, name="by_entry", tag="by_entry", bufs=HALVES)
                nc.scalar.copy(by_entry[:], summed[:])
                by_row = psum.tile([P, BLOCKS, P], F32, name="by_row", tag="bank%d" % half)
                for b in range(BLOCKS):
                    nc.tensor.transpose(by_row[:, b, :], by_entry[:, b, :], ident[:])
                nc.scalar.copy(h[:, half_cols(half)], by_row[:].rearrange("p b j -> p (b j)"))

        h0 = [sb.tile([P, BANK], F32, name="h0", tag="out%d" % half)[:] for half in range(HALVES)]
        gated_product(0, 0, quantise_w2(0), h0)
        nc.vector.tensor_tensor(h0[0], h0[0], tide_sb[:, half_cols(0)], ALU.add)
        nc.vector.tensor_tensor(page[0][:].indirect(half_list(idx2, 0)), h0[0], wgs_sb[:, half_cols(0)], ALU.mult)
        w2_q = quantise_w2(1)
        nc.vector.tensor_tensor(h0[1], h0[1], tide_sb[:, half_cols(1)], ALU.add)
        nc.vector.tensor_tensor(page[0][:].indirect(half_list(idx2, 1)), h0[1], wgs_sb[:, half_cols(1)], ALU.mult)
        u1 = sb.tile([P, S], F32, name="u1", tag="tab1", align_bytes=64)
        gated_product(1, 1, w2_q, [u1[:, half_cols(half)] for half in range(HALVES)])
        w2_q = quantise_w2(2)
        h1 = sb.tile([P, S], F32, name="h1", tag="bf%d" % (PASSES - 1), align_bytes=64)
        nc.vector.tensor_tensor(h1[:], u1[:], tide_sb[:, S : 2 * S], ALU.add)
        u23 = sb.tile([P, 2 * S], F32, name="u23", tag="tab0", align_bytes=64)
        h23 = sb.tile([P, 2 * S], F32, name="h23", tag="h_or_reread")
        u_late = {c: u23[:, (c - 2) * S : (c - 1) * S] for c in range(2, TILES)}
        h_late = {c: h23[:, (c - 2) * S : (c - 1) * S] for c in range(2, TILES)}
        for c in range(2, TILES):
            gated_product(c, 2, w2_q, [u_late[c][:, half_cols(half)] for half in range(HALVES)])
        for c in range(2, TILES):
            add_tide_by_transposes(c, u_late[c], h_late[c])
        nc.vector.tensor_tensor(page[1][:].indirect(idx2[:]), h1[:], wgs_sb[:], ALU.mult)
        for c in range(2, TILES):
            nc.vector.tensor_tensor(page[c][:].indirect(idx2[:]), h_late[c], wgs_sb[:], ALU.mult)

        turned = psum.tile([P, P], F32, name="turned", tag="bank6")
        nc.tensor.transpose(turned[:], vectors[:], ident[:])
        factors = sb.tile([P, 2 * TILES], F32, name="factors")
        nc.scalar.copy(factors[:], turned[:, 0 : 2 * TILES])
        w3_codes, w3_scales = quantise(w3_raw[:], "w3", nc.scalar.copy, "bf0")

        def bar_of(c):
            return factors[:, TILES + c : TILES + c + 1]

        x = [sb.tile([P, BANK, PACK], BF16, name="x", tag="x%d" % half, align_bytes=64) for half in range(HALVES)]
        reread = sb.tile([P, (2 * TILES - 1) * M], F32, name="reread", tag="h_or_reread")
        sandbar = {}

        def reread_bathers(half):
            by_cell = [
                psum.tile([P, H], BF16, name="by_cell", tag="bank%d" % (BLOCKS * half + b)) for b in range(BLOCKS)
            ]
            for c in range(TILES):
                cells = reread[:, (half * TILES + c) * BANK : (half * TILES + c + 1) * BANK]
                nc.vector.tensor_copy(cells, page[c][:].indirect(half_list(idx3, half)))
                rounded = sb.tile([P, BANK], BF16, name="rounded", tag="rounded", bufs=3)
                nc.scalar.activation(rounded[:], cells, ACT.Abs, scale=factors[:, c : c + 1])
                for b in range(BLOCKS):
                    nc.tensor.transpose(by_cell[b][:, c * P : (c + 1) * P], rounded[:, b * P : (b + 1) * P], ident_bf[:])
            x_words = x[half][:].rearrange("p m i -> p (m i)").bitcast(F32)
            for pair in range(BLOCKS // 2):
                carried = psum.tile([P, 2, 2, P], F32, name="carried", tag="bank%d" % (2 * half + pair))
                for e in range(2):
                    b = 2 * pair + e
                    if (half, b) == (HALVES - 1, BLOCKS - 1):
                        words = sb.tile([P, 2, P], F32, name="words", tag="tide_or_gate")
                    else:
                        words = sb.tile([P, 2, P], F32, name="words", tag="words", bufs=BLOCKS)
                    nc.scalar.copy(words[:], by_cell[b][:].bitcast(F32).rearrange("m (p u) -> m u p", u=2))
                    for u in range(2):
                        nc.tensor.transpose(carried[:, e, u, :], words[:, u, :], ident[:])
                nc.scalar.copy(
                    x_words[:, pair * BANK : (pair + 1) * BANK].rearrange("p (e m u) -> p e m u", e=2, u=2),
                    carried[:].rearrange("p e u m -> p e m u"),
                )

        def reread_sandbar(c, cells):
            sandbar[c] = cells
            nc.vector.tensor_copy(cells, page[c][:].indirect(idx4[:]))

        for half in range(HALVES):
            reread_bathers(half)
        for c in range(TILES - 1):
            reread_sandbar(c, reread[:, (TILES + c) * M : (TILES + c + 1) * M])

        x_q, x_s = [], []
        for half in range(HALVES):
            x_q.append(sb.tile([P, BANK], U32, name="x_q%d" % half, align_bytes=64))
            x_s.append(sb.tile([P, BANK], U8, name="x_s%d" % half, align_bytes=64))
            nc.vector.quantize_mx(
                out=x_q[half][:].bitcast(FP8X4), scales=x_s[half][:], in_=x[half][:].rearrange("p m i -> p (m i)")
            )
        reread_sandbar(TILES - 1, sb.tile([P, M], F32, name="sandbar_last", tag="x0", align_bytes=64)[:])

        gates = sb.tile([P, TILES * M], F32, name="gates", tag="tide_or_gate")
        pieces = [(c, half) for half in range(HALVES) for c in range(TILES)]
        gate, sand = {}, {}
        for c, half in pieces:
            gate[c, half] = gates[:, (half * TILES + c) * BANK : (half * TILES + c + 1) * BANK]
            nc.scalar.activation(gate[c, half], sandbar[c][:, half_cols(half)], ACT.Sigmoid, scale=bar_of(c))
        for c, half in pieces[:GPSIMD_SUMS]:
            sand[c, half] = sb.tile([P, BANK], F32, name="sand", tag="th_or_sand", bufs=TILES * HALVES)
            nc.scalar.activation(sand[c, half][:], sandbar[c][:, half_cols(half)], ACT.Copy, scale=bar_of(c))
        res = [sb.tile([P, TILES * BANK], F32, name="res", tag="out%d" % half) for half in range(HALVES)]
        for c, half in pieces:
            y = psum.tile([P, BANK], F32, name="y", tag="bank%d" % (TILES * (1 - half) + c))
            nc.tensor.matmul_mx(
                out=y[:],
                lhsT=w3_codes[:, c * P : (c + 1) * P].bitcast(FP8X4),
                lhsT_scale=w3_scales[:, c * P : (c + 1) * P],
                rhs=x_q[half][:].bitcast(FP8X4),
                rhs_scale=x_s[half][:],
                start=True,
                stop=True,
            )
            nc.vector.tensor_tensor(res[half][:, c * BANK : (c + 1) * BANK], y[:], gate[c, half], ALU.mult)
        for c, half in pieces[:GPSIMD_SUMS]:
            gated = res[half][:, c * BANK : (c + 1) * BANK]
            nc.gpsimd.tensor_tensor(gated, gated, sand[c, half][:], ALU.add)
            nc.sync.dma_start(out=out[c * P : (c + 1) * P, half_cols(half)], in_=gated)
        for c, half in pieces[GPSIMD_SUMS:]:
            parts = 2 if (c, half) == pieces[-1] else 1
            width = BANK // parts
            for m0 in range(0, BANK, width):
                gated = res[half][:, c * BANK + m0 : c * BANK + m0 + width]
                cols = slice(half * BANK + m0, half * BANK + m0 + width)
                nc.vector.scalar_tensor_tensor(gated, sandbar[c][:, cols], bar_of(c), gated, ALU.mult, ALU.add)
                nc.sync.dma_start(out=out[c * P : (c + 1) * P, cols], in_=gated)
